import numpy as np, ml_dtypes
CORES = [3,67,11,75,19,83,27,91,35,99,43,107,51,115,59,123]
N = 16
def setup_inputs(rng):
    return {"x": rng.standard_normal((N, 128, 2048), dtype=np.float32).astype(ml_dtypes.bfloat16)}
def reference(x):
    s = x.sum(axis=0, dtype=np.float64).astype(x.dtype)
    b = 2048 // N
    return {"y": np.stack([s[:, r * b:(r + 1) * b] for r in range(N)])}

@@ -1,0 +1,93 @@
+from concourse.bass import DstId, RemoteDMATransfer
+
+SCRATCH = {
+    "st": ("dram", [32, 128, 64], "bfloat16"),
+    "ml": ("dram", [16, 128, 64], "bfloat16"),
+    "pl": ("dram", [16, 128, 64], "bfloat16"),
+    "res": ("dram", [2, 128, 64], "bfloat16"),
+}
+SEMAPHORES = ["ld_t", "ld_m", "got_t", "got_m", "mate", "plane", "fin", "sent", "stored"]
+
+BLK = 128
+
+
+def rank_program(g, core, T, topo):
+    c, k_core = divmod(core, 8)
+    if k_core not in (2, 3, 7):
+        return
+    par = c & 1
+    mate = c ^ 1
+    S = T.sem
+
+    def dst(core_to):
+        rid, pid, _se = topo.addr(core_to)
+        return DstId(rid=rid, pnc=pid)
+
+    def copy(src, out, to, eng, sem):
+        return RemoteDMATransfer(dst_ids=[dst(to)], dma_engine_mask=eng, remote_sem=sem, src=src, dst=out)
+
+    def fold(srcs, out, to, eng, sem):
+        return RemoteDMATransfer(dst_ids=[dst(to)], dma_engine_mask=eng, remote_sem=sem, srcs=srcs, dsts=[out],
+                                 alu_op=1)
+
+    R, H, Q = 8 * c + 3, 8 * c + 2, 8 * c + 7
+    theirs = [2 * k + (1 - par) for k in range(8)]
+    mine = [2 * k + par for k in range(8)]
+
+    if core == H:
+        g.wait_ge(S.plane, 8)
+        g.remote_dma_fused([fold([T.pl[2 * k] for k in range(8)], T.res[0], R, 0xFFFF, S.fin)], local_sem=S.sent)
+        g.wait_ge(S.sent, 16)
+        return
+
+    h = 0 if core == R else 1
+    sent = 0
+
+    if core == R:
+        for sem, chips in ((S.ld_t, theirs), (S.ld_m, mine)):
+            for i, d in enumerate(chips):
+                r = T.rank_of(8 * d + 3)
+                q = g.sync if i % 2 == 0 else g.scalar
+                q.dma_start(T.st[2 * d:2 * d + 2], T.x[:, BLK * r:BLK * (r + 1)]).then_inc(sem, 16)
+        g.wait_ge(S.ld_t, 128)
+        g.remote_dma_fused([copy(T.st[2 * d + 1], T.st[2 * d + 1], Q, 1 << (8 + k), S.got_t)
+                            for k, d in enumerate(theirs)], local_sem=S.sent)
+        sent += 8
+    else:
+        g.wait_ge(S.got_t, 8)
+
+    g.remote_dma_fused([copy(T.st[2 * d + h], T.ml[2 * k + h], 8 * mate + k_core, 1 << k, S.mate)
+                        for k, d in enumerate(theirs)], local_sem=S.sent)
+    sent += 8
+
+    if core == R:
+        g.wait_ge(S.ld_m, 128)
+        g.remote_dma_fused([copy(T.st[2 * d + 1], T.st[2 * d + 1], Q, 1 << (8 + k), S.got_m)
+                            for k, d in enumerate(mine)], local_sem=S.sent)
+        sent += 8
+    else:
+        g.wait_ge(S.got_m, 8)
+    g.wait_ge(S.mate, 8)
+
+    trs = []
+    for k, d in enumerate(mine):
+        if d == c and h == 1:
+            continue
+        to = 8 * d + (2 if h == 0 else 7)
+        trs.append(fold([T.st[2 * d + h], T.ml[2 * k + h]], T.pl[2 * (c >> 1) + h], to, 1 << k, S.plane))
+    g.remote_dma_fused(trs, local_sem=S.sent)
+    sent += len(trs)
+
+    if core == Q:
+        g.wait_ge(S.plane, 7)
+        srcs = [T.pl[2 * k + 1] for k in range(8) if k != (c >> 1)]
+        srcs += [T.st[2 * c + 1], T.ml[2 * (c >> 1) + 1]]
+        g.remote_dma_fused([fold(srcs, T.res[1], R, 0xFFFF, S.fin)], local_sem=S.sent)
+        sent += 16
+        g.wait_ge(S.sent, sent)
+        return
+
+    g.wait_ge(S.fin, 32)
+    g.dma_start(T.y[:, :], T.res[:]).then_inc(S.stored, 16)
+    g.wait_ge(S.stored, 16)
+    g.wait_ge(S.sent, sent)

@@ -1,22 +1,26 @@
 from concourse.bass import DstId, RemoteDMATransfer
 
-SCRATCH = {
-    "st": ("dram", [32, 128, 64], "bfloat16"),
-    "ml": ("dram", [16, 128, 64], "bfloat16"),
-    "pl": ("dram", [16, 128, 64], "bfloat16"),
-    "res": ("dram", [2, 128, 64], "bfloat16"),
-}
-SEMAPHORES = ["ld_t", "ld_m", "got_t", "got_m", "mate", "plane", "fin", "sent", "stored"]
-
+A = 82
+G = 128 - A
 BLK = 128
+
+SCRATCH = {
+    "sa": ("dram", [16, 128, A], "bfloat16"),
+    "ma": ("dram", [8, 128, A], "bfloat16"),
+    "pa": ("dram", [8, 128, A], "bfloat16"),
+    "ra": ("dram", [128, A], "bfloat16"),
+    "sg": ("dram", [16, 128, G], "bfloat16"),
+    "lg": ("dram", [16, 128, G], "bfloat16"),
+    "rg": ("dram", [128, G], "bfloat16"),
+}
+SEMAPHORES = ["ld_at", "ld_gt", "ld_gm", "ld_am", "got", "mate", "plane", "land", "fin_a", "fin_g", "sent", "stored"]
 
 
 def rank_program(g, core, T, topo):
     c, k_core = divmod(core, 8)
-    if k_core not in (2, 3, 7):
+    if k_core not in (2, 3, 6, 7):
         return
     par = c & 1
-    mate = c ^ 1
     S = T.sem
 
     def dst(core_to):
@@ -30,64 +34,55 @@ def rank_program(g, core, T, topo):
         return RemoteDMATransfer(dst_ids=[dst(to)], dma_engine_mask=eng, remote_sem=sem, srcs=srcs, dsts=[out],
                                  alu_op=1)
 
-    R, H, Q = 8 * c + 3, 8 * c + 2, 8 * c + 7
+    R, QM, QT = 8 * c + 3, 8 * c + 6, 8 * c + 7
     theirs = [2 * k + (1 - par) for k in range(8)]
     mine = [2 * k + par for k in range(8)]
 
-    if core == H:
+    if k_core == 2:
         g.wait_ge(S.plane, 8)
-        g.remote_dma_fused([fold([T.pl[2 * k] for k in range(8)], T.res[0], R, 0xFFFF, S.fin)], local_sem=S.sent)
+        g.remote_dma_fused([fold([T.pa[k] for k in range(8)], T.ra[:], R, 0xFFFF, S.fin_a)], local_sem=S.sent)
         g.wait_ge(S.sent, 16)
         return
 
-    h = 0 if core == R else 1
-    sent = 0
-
-    if core == R:
-        for sem, chips in ((S.ld_t, theirs), (S.ld_m, mine)):
-            for i, d in enumerate(chips):
-                r = T.rank_of(8 * d + 3)
-                q = g.sync if i % 2 == 0 else g.scalar
-                q.dma_start(T.st[2 * d:2 * d + 2], T.x[:, BLK * r:BLK * (r + 1)]).then_inc(sem, 16)
-        g.wait_ge(S.ld_t, 128)
-        g.remote_dma_fused([copy(T.st[2 * d + 1], T.st[2 * d + 1], Q, 1 << (8 + k), S.got_t)
-                            for k, d in enumerate(theirs)], local_sem=S.sent)
-        sent += 8
-    else:
-        g.wait_ge(S.got_t, 8)
-
-    g.remote_dma_fused([copy(T.st[2 * d + h], T.ml[2 * k + h], 8 * mate + k_core, 1 << k, S.mate)
-                        for k, d in enumerate(theirs)], local_sem=S.sent)
-    sent += 8
-
-    if core == R:
-        g.wait_ge(S.ld_m, 128)
-        g.remote_dma_fused([copy(T.st[2 * d + 1], T.st[2 * d + 1], Q, 1 << (8 + k), S.got_m)
-                            for k, d in enumerate(mine)], local_sem=S.sent)
-        sent += 8
-    else:
-        g.wait_ge(S.got_m, 8)
-    g.wait_ge(S.mate, 8)
-
-    trs = []
-    for k, d in enumerate(mine):
-        if d == c and h == 1:
-            continue
-        to = 8 * d + (2 if h == 0 else 7)
-        trs.append(fold([T.st[2 * d + h], T.ml[2 * k + h]], T.pl[2 * (c >> 1) + h], to, 1 << k, S.plane))
-    g.remote_dma_fused(trs, local_sem=S.sent)
-    sent += len(trs)
-
-    if core == Q:
-        g.wait_ge(S.plane, 7)
-        srcs = [T.pl[2 * k + 1] for k in range(8) if k != (c >> 1)]
-        srcs += [T.st[2 * c + 1], T.ml[2 * (c >> 1) + 1]]
-        g.remote_dma_fused([fold(srcs, T.res[1], R, 0xFFFF, S.fin)], local_sem=S.sent)
-        sent += 16
-        g.wait_ge(S.sent, sent)
+    if k_core == 7:
+        g.wait_ge(S.got, 8)
+        g.remote_dma_fused([copy(T.sg[d], T.lg[c], 8 * d + 6, 1 << k, S.land) for k, d in enumerate(theirs)],
+                           local_sem=S.sent)
+        g.wait_ge(S.sent, 8)
         return
 
-    g.wait_ge(S.fin, 32)
-    g.dma_start(T.y[:, :], T.res[:]).then_inc(S.stored, 16)
-    g.wait_ge(S.stored, 16)
-    g.wait_ge(S.sent, sent)
+    if k_core == 6:
+        g.wait_ge(S.got, 8)
+        g.remote_dma_fused([copy(T.sg[d], T.lg[c], 8 * d + 6, 1 << k, S.land) for k, d in enumerate(mine) if d != c],
+                           local_sem=S.sent)
+        g.wait_ge(S.land, 15)
+        g.remote_dma_fused([fold([T.sg[c]] + [T.lg[s] for s in range(16) if s != c], T.rg[:], R, 0xFFFF, S.fin_g)],
+                           local_sem=S.sent)
+        g.wait_ge(S.sent, 7 + 16)
+        return
+
+    for sem, chips, buf, lo, hi in ((S.ld_at, theirs, T.sa, 0, A), (S.ld_gt, theirs, T.sg, A, 128),
+                                    (S.ld_gm, mine, T.sg, A, 128), (S.ld_am, mine, T.sa, 0, A)):
+        for i, d in enumerate(chips):
+            r = T.rank_of(8 * d + 3)
+            q = g.sync if i % 2 == 0 else g.scalar
+            q.dma_start(buf[d], T.x[lo:hi, BLK * r:BLK * (r + 1)]).then_inc(sem, 16)
+    g.wait_ge(S.ld_at, 128)
+    g.remote_dma_fused([copy(T.sa[d], T.ma[k], 8 * (c ^ 1) + 3, 1 << k, S.mate) for k, d in enumerate(theirs)],
+                       local_sem=S.sent)
+    g.wait_ge(S.ld_gt, 128)
+    g.remote_dma_fused([copy(T.sg[d], T.sg[d], QT, 1 << (8 + k), S.got) for k, d in enumerate(theirs)],
+                       local_sem=S.sent)
+    g.wait_ge(S.ld_gm, 128)
+    g.remote_dma_fused([copy(T.sg[d], T.sg[d], QM, 1 << (8 + k), S.got) for k, d in enumerate(mine)],
+                       local_sem=S.sent)
+    g.wait_ge(S.ld_am, 128)
+    g.wait_ge(S.mate, 8)
+    g.remote_dma_fused([fold([T.sa[d], T.ma[k]], T.pa[c >> 1], 8 * d + 2, 1 << k, S.plane)
+                        for k, d in enumerate(mine)], local_sem=S.sent)
+    g.sync.wait_ge(S.fin_a, 16)
+    g.sync.dma_start(T.y[0:A, :], T.ra[:]).then_inc(S.stored, 16)
+    g.scalar.wait_ge(S.fin_g, 16)
+    g.scalar.dma_start(T.y[A:128, :], T.rg[:]).then_inc(S.stored, 16)
+    g.wait_ge(S.stored, 32)
+    g.wait_ge(S.sent, 32)

from concourse.bass import DstId, RemoteDMATransfer

A = 82
G = 128 - A
BLK = 128

SCRATCH = {
    "sa": ("dram", [16, 128, A], "bfloat16"),
    "ma": ("dram", [8, 128, A], "bfloat16"),
    "pa": ("dram", [8, 128, A], "bfloat16"),
    "ra": ("dram", [128, A], "bfloat16"),
    "sg": ("dram", [16, 128, G], "bfloat16"),
    "lg": ("dram", [16, 128, G], "bfloat16"),
    "rg": ("dram", [128, G], "bfloat16"),
}
SEMAPHORES = ["ld_at", "ld_gt", "ld_gm", "ld_am", "got", "mate", "plane", "land", "fin_a", "fin_g", "sent", "stored"]


def rank_program(g, core, T, topo):
    c, k_core = divmod(core, 8)
    if k_core not in (2, 3, 6, 7):
        return
    par = c & 1
    S = T.sem

    def dst(core_to):
        rid, pid, _se = topo.addr(core_to)
        return DstId(rid=rid, pnc=pid)

    def copy(src, out, to, eng, sem):
        return RemoteDMATransfer(dst_ids=[dst(to)], dma_engine_mask=eng, remote_sem=sem, src=src, dst=out)

    def fold(srcs, out, to, eng, sem):
        return RemoteDMATransfer(dst_ids=[dst(to)], dma_engine_mask=eng, remote_sem=sem, srcs=srcs, dsts=[out],
                                 alu_op=1)

    R, QM, QT = 8 * c + 3, 8 * c + 6, 8 * c + 7
    theirs = [2 * k + (1 - par) for k in range(8)]
    mine = [2 * k + par for k in range(8)]

    if k_core == 2:
        g.wait_ge(S.plane, 8)
        g.remote_dma_fused([fold([T.pa[k] for k in range(8)], T.ra[:], R, 0xFFFF, S.fin_a)], local_sem=S.sent)
        g.wait_ge(S.sent, 16)
        return

    if k_core == 7:
        g.wait_ge(S.got, 8)
        g.remote_dma_fused([copy(T.sg[d], T.lg[c], 8 * d + 6, 1 << k, S.land) for k, d in enumerate(theirs)],
                           local_sem=S.sent)
        g.wait_ge(S.sent, 8)
        return

    if k_core == 6:
        g.wait_ge(S.got, 8)
        g.remote_dma_fused([copy(T.sg[d], T.lg[c], 8 * d + 6, 1 << k, S.land) for k, d in enumerate(mine) if d != c],
                           local_sem=S.sent)
        g.wait_ge(S.land, 15)
        g.remote_dma_fused([fold([T.sg[c]] + [T.lg[s] for s in range(16) if s != c], T.rg[:], R, 0xFFFF, S.fin_g)],
                           local_sem=S.sent)
        g.wait_ge(S.sent, 7 + 16)
        return

    for sem, chips, buf, lo, hi in ((S.ld_at, theirs, T.sa, 0, A), (S.ld_gt, theirs, T.sg, A, 128),
                                    (S.ld_gm, mine, T.sg, A, 128), (S.ld_am, mine, T.sa, 0, A)):
        for i, d in enumerate(chips):
            r = T.rank_of(8 * d + 3)
            q = g.sync if i % 2 == 0 else g.scalar
            q.dma_start(buf[d], T.x[lo:hi, BLK * r:BLK * (r + 1)]).then_inc(sem, 16)
    g.wait_ge(S.ld_at, 128)
    g.remote_dma_fused([copy(T.sa[d], T.ma[k], 8 * (c ^ 1) + 3, 1 << k, S.mate) for k, d in enumerate(theirs)],
                       local_sem=S.sent)
    g.wait_ge(S.ld_gt, 128)
    g.remote_dma_fused([copy(T.sg[d], T.sg[d], QT, 1 << (8 + k), S.got) for k, d in enumerate(theirs)],
                       local_sem=S.sent)
    g.wait_ge(S.ld_gm, 128)
    g.remote_dma_fused([copy(T.sg[d], T.sg[d], QM, 1 << (8 + k), S.got) for k, d in enumerate(mine)],
                       local_sem=S.sent)
    g.wait_ge(S.ld_am, 128)
    g.wait_ge(S.mate, 8)
    g.remote_dma_fused([fold([T.sa[d], T.ma[k]], T.pa[c >> 1], 8 * d + 2, 1 << k, S.plane)
                        for k, d in enumerate(mine)], local_sem=S.sent)
    g.sync.wait_ge(S.fin_a, 16)
    g.sync.dma_start(T.y[0:A, :], T.ra[:]).then_inc(S.stored, 16)
    g.scalar.wait_ge(S.fin_g, 16)
    g.scalar.dma_start(T.y[A:128, :], T.rg[:]).then_inc(S.stored, 16)
    g.wait_ge(S.stored, 32)
    g.wait_ge(S.sent, 32)
